import numpy as np
import ml_dtypes


def mxq(x, axis, fmt="e4m3"):
    dtype, down = {"e4m3": (ml_dtypes.float8_e4m3fn, 7), "e5m2": (ml_dtypes.float8_e5m2, 14)}[fmt]
    v = np.moveaxis(np.asarray(x, np.float32).astype(ml_dtypes.bfloat16).astype(np.float64), axis, -1)
    blocks = v.reshape(v.shape[:-1] + (-1, 32))
    amax = np.abs(blocks).max(-1, keepdims=True)
    byte = np.maximum(np.where(amax > 0, np.frexp(amax)[1] - 1 + 127, 0) - down, 1)
    scale = np.exp2(byte - 127.0)
    codes = (blocks / scale).astype(np.float32).astype(dtype).astype(np.float64)
    return np.moveaxis((codes * scale).reshape(v.shape), -1, axis)


WIDE = False


def mx_kscale(k):
    if not WIDE:
        return np.ones(k)
    levels = np.array([10, -10, 5, -5, 0])
    if k % 512:
        return np.exp2(np.random.permutation(np.resize(levels, k // 32))).repeat(32)
    a = np.empty((k // 512, 16))
    for p in range(k // 512):
        a[p, :8] = np.random.permutation(np.resize(levels, 8))
        for g in range(8):
            far = levels[np.abs(levels - a[p, g]) >= 10]
            a[p, g + 8] = far[np.random.randint(len(far))]
    return np.exp2(a.ravel()).repeat(32)


def f64(x):
    return np.asarray(x).astype(np.float64)


def striped(idx):
    return np.tile(idx.reshape(-1, 16).T, (8, 1)).astype(np.uint16)


def unstriped(offs):
    return offs[:16].T.reshape(-1).astype(np.int64)


E2M1 = np.array([0.0, 0.5, 1.0, 1.5, 2.0, 3.0, 4.0, 6.0, -0.0, -0.5, -1.0, -1.5, -2.0, -3.0, -4.0, -6.0])


def pack_weight(w, fmt):
    k, n = w.shape
    w = f64(np.asarray(w, np.float32).astype(ml_dtypes.bfloat16)).reshape(k // 32, 32, n)
    amax = np.abs(w).max(1)
    if fmt == "e4m3":
        byte = np.frexp(amax)[1] - 1 + 127 - 7
    else:
        mant, ex = np.frexp(amax / 6.0)
        byte = np.where(mant > 0.5, ex, ex - 1) + 127
    byte = np.clip(np.where(amax > 0, byte, 1), 1, 254)
    scaled = (w * np.exp2(127.0 - byte)[:, None, :]).reshape(k, n).astype(np.float32)
    by_word = np.ascontiguousarray(scaled.reshape(k // 512, 128, 4, n).transpose(0, 1, 3, 2))
    if fmt == "e4m3":
        words = by_word.astype(ml_dtypes.float8_e4m3fn).view(np.uint8)
    else:
        c = by_word.astype(ml_dtypes.float4_e2m1fn).view(np.uint8) & 0xF
        words = (c[..., 0::2] | (c[..., 1::2] << 4)).reshape(k // 512, 128, 2 * n)
    return np.ascontiguousarray(words), np.ascontiguousarray(byte.astype(np.uint8).reshape(k // 512, 16, n))


def unpack_weight(words, scales, fmt):
    g, _, n = scales.shape
    words = np.ascontiguousarray(words).reshape(g, 128, n, -1)
    if fmt == "e4m3":
        vals = words.view(ml_dtypes.float8_e4m3fn).astype(np.float64)
    else:
        nib = np.empty((g, 128, n, 4), np.uint8)
        nib[..., 0::2] = words & 0xF
        nib[..., 1::2] = words >> 4
        vals = E2M1[nib]
    vals = vals * np.repeat(np.exp2(scales.astype(np.float64) - 127.0), 8, axis=1)[..., None]
    return vals.transpose(0, 1, 3, 2).reshape(g * 512, n)


def gelu(v):
    return 0.5 * v * (1.0 + np.tanh(np.sqrt(2.0 / np.pi) * (v + 0.044715 * v**3)))


def striped8(idx):
    return np.concatenate([v.reshape(-1, 16).T for v in idx]).astype(np.uint16)


def unstriped8(offs):
    return np.stack([offs[16 * g:16 * g + 16].T.reshape(-1) for g in range(8)]).astype(np.int64)


def heads(h, wgt, idx8):
    r = np.arange(h.shape[0])
    return wgt[r // 4 % 128] * h[r[:, None], idx8[r % 512 // 64]]


K, H, N, T, S, P = 512, 1024, 512, 4096, 1024, 512

def setup_inputs():
    n = np.random.standard_normal
    s = mx_kscale(K)[:, None]
    u = mx_kscale(H)[:, None]
    tab_words, tab_scales = pack_weight(n((K, T)) * s, "e4m3")
    w1 = 0.9 * n((K, H)) / np.sqrt(K) / s * u.T
    w2_words, w2_scales = pack_weight(0.9 * n((K, H)) / np.sqrt(K) / s, "e2m1")
    w3 = 0.7 * n((K, H)) / np.sqrt(K) / s * u.T
    w4 = 0.8 * n((H, N)) / np.sqrt(H) / u
    w5_words, w5_scales = pack_weight(0.5 * n((H, N)) / np.sqrt(H) / u**2, "e4m3")
    wga = np.repeat(np.random.uniform(0.5, 2.0, (8, P)), 16, axis=0)
    wgb = np.repeat(np.random.uniform(0.5, 2.0, (8, P)), 16, axis=0)
    return {"tab_words": tab_words, "tab_scales": tab_scales,
            "offs": striped(np.random.permutation(T)[:S]),
            "w1": w1.astype(np.float32), "w2_words": w2_words, "w2_scales": w2_scales,
            "w3": w3.astype(np.float32),
            "offs2": striped8(np.stack([np.random.permutation(S)[:P] for _ in range(8)])),
            "offs3": striped8(np.stack([np.random.permutation(S)[:P] for _ in range(8)])),
            "wga": wga.astype(np.float32), "wgb": wgb.astype(np.float32),
            "w4": w4.astype(np.float32), "w5_words": w5_words, "w5_scales": w5_scales,
            "b": (0.5 * n(N)).astype(np.float32)}

def reference(tab_words, tab_scales, offs, w1, w2_words, w2_scales, w3, offs2, offs3, wga, wgb, w4, w5_words, w5_scales, b):
    v = unpack_weight(tab_words, tab_scales, "e4m3")[:, unstriped(offs)]
    h1 = mxq(f64(w1), 0, "e4m3").T @ v
    h2 = unpack_weight(w2_words, w2_scales, "e2m1").T @ v
    h3 = mxq(f64(w3), 0, "e4m3").T @ v
    h = h1 * h2 + h3
    xa = heads(h, f64(wga), unstriped8(offs2))
    xb = heads(h, f64(wgb), unstriped8(offs3))
    zm = mxq(np.maximum(xa, xb), 0, "e4m3")
    zp = mxq(xa * xb, 0, "e4m3")
    y = mxq(f64(w4), 0, "e4m3").T @ zm + unpack_weight(w5_words, w5_scales, "e4m3").T @ zp
    y = y + f64(b)[:, None]
    return 0.5 * y * (1.0 + np.tanh(0.7978845608 * (y + 0.044715 * y**3)))

@@ -1,0 +1,263 @@
+from contextlib import ExitStack
+
+import concourse.mybir as mybir
+from concourse.masks import make_identity
+
+K, H, N, T, S, M = 512, 1024, 512, 4096, 1024, 512
+FLOPS = 2 * K * H * S * 3 + 2 * H * N * M * 2
+
+F32 = mybir.dt.float32
+BF16 = mybir.dt.bfloat16
+I32 = mybir.dt.int32
+U32 = mybir.dt.uint32
+U16 = mybir.dt.uint16
+U8 = mybir.dt.uint8
+E4M3 = mybir.dt.float8_e4m3fn_x4
+E2M1 = mybir.dt.float4_e2m1fn_x4
+MULT = mybir.AluOpType.mult
+ADD = mybir.AluOpType.add
+MAX = mybir.AluOpType.max
+GELU = mybir.ActivationFunctionType.Gelu_apprx_tanh
+
+P = 128
+PACK = 4
+PASS = P * PACK
+BANK = 512
+
+
+def tile_list_mycorrhiza_transfer_score_kernel(
+    tc, tab_words, tab_scales, offs, w1, w2_words, w2_scales, w3, offs2, offs3, wga, wgb, w4, w5_words, w5_scales, b, out
+):
+    nc = tc.nc
+    with ExitStack() as ctx:
+        keep = ctx.enter_context(tc.tile_pool(name="keep", bufs=1))
+        ring = ctx.enter_context(tc.tile_pool(name="ring", bufs=2))
+        raws = ctx.enter_context(tc.tile_pool(name="raws", bufs=2))
+        psum = ctx.enter_context(tc.psum_pool(name="psum", bufs=2))
+
+        def held(name, shape, dtype):
+            return keep.tile(shape, dtype, name=name, align_bytes=64)
+
+        def load_scale_rows(queue, plane, rows):
+            for q in range(4):
+                queue.dma_start(out=plane[32 * q : 32 * q + 4], in_=rows[4 * q : 4 * q + 4])
+
+        def load_raw(rows):
+            raw = raws.tile([P, PACK, BANK], F32, name="raw")
+            nc.sync.dma_start(out=raw[:], in_=rows.rearrange("(p j) c -> p j c", j=PACK))
+            return raw
+
+        def round_plain(raw):
+            grouped = ring.tile([P, BANK, PACK], BF16, name="grouped", align_bytes=64)
+            nc.scalar.copy(
+                out=grouped[:].rearrange("p (c i) j -> p c j i", i=4),
+                in_=raw[:].rearrange("p j (c i) -> p c j i", i=4),
+            )
+            return grouped
+
+        def round_dealt(raw, name):
+            grouped = held(name, [P, BANK, PACK], BF16)
+            nc.scalar.copy(
+                out=grouped[:].rearrange("p (t m) j -> p m j t", t=PACK),
+                in_=raw[:].rearrange("p j (m t) -> p m j t", t=PACK),
+            )
+            return grouped
+
+        def quantise(name, grouped):
+            codes = held(name + "_codes", [P, BANK], U32)
+            scales = held(name + "_scales", [P, BANK], U8)
+            nc.vector.quantize_mx(
+                out=codes[:].bitcast(E4M3), scales=scales[:], in_=grouped[:].rearrange("p c j -> p (c j)")
+            )
+            return codes, scales
+
+        idx = held("idx", [P, S // 16], U16)
+        idx2 = held("idx2", [P, M // 16], U16)
+        idx3 = held("idx3", [P, M // 16], U16)
+        tab_w = held("tab_w", [P, T], I32)
+        tab_s = held("tab_s", [P, T // 4], I32)
+        w2_w = held("w2_w", [P, 2 * H // 4], I32)
+        w2_s = held("w2_s", [P, H // 4], I32)
+        ident = held("ident", [P, P], F32)
+
+        nc.vector.memset(tab_s[:], 0)
+        nc.gpsimd.memset(w2_s[:], 0)
+        load_scale_rows(nc.gpsimd, w2_s, w2_scales[0].bitcast(I32))
+        make_identity(nc, ident[:])
+        nc.sync.dma_start(out=idx[:], in_=offs)
+        nc.sync.dma_start(out=idx2[:], in_=offs2)
+        nc.sync.dma_start(out=idx3[:], in_=offs3)
+        nc.sync.dma_start(out=w2_w[:], in_=w2_words[0].bitcast(I32))
+        w1_raw0 = load_raw(w1[:, 0:BANK])
+        w3_raw0 = load_raw(w3[:, 0:BANK])
+        nc.sync.dma_start(out=tab_w[:], in_=tab_words[0].rearrange("p t i -> p (t i)").bitcast(I32))
+        load_scale_rows(nc.scalar, tab_s, tab_scales[0].bitcast(I32))
+
+        v_s = held("v_s", [P, S], U8)
+        nc.vector.tensor_copy(out=v_s[:], in_=tab_s[:].bitcast(U8).indirect(idx[:]))
+
+        w2_dealt_w = held("w2_dealt_w", [P, BANK], U16)
+        w2_dealt_s = held("w2_dealt_s", [P, BANK], U8)
+        nc.vector.tensor_copy(
+            out=w2_dealt_w[:].rearrange("p (t m) -> p t m", t=PACK),
+            in_=w2_w[:].bitcast(U16)[:, 0:BANK].rearrange("p (m t) -> p t m", t=PACK),
+        )
+        nc.vector.tensor_copy(
+            out=w2_dealt_s[:].rearrange("p (t m) -> p t m", t=PACK),
+            in_=w2_s[:].bitcast(U8)[:, 0:BANK].rearrange("p (m t) -> p t m", t=PACK),
+        )
+        w1_q0 = quantise("w1_0", round_dealt(w1_raw0, "w1_dealt"))
+        w3_q0 = quantise("w3_0", round_dealt(w3_raw0, "w3_dealt"))
+
+        v_w = [held("v_w%d" % u, [P, BANK], U32) for u in range(2)]
+        for u in range(2):
+            nc.vector.tensor_copy(out=v_w[u][:], in_=tab_w[:].bitcast(U32).indirect(idx[:, 32 * u : 32 * u + 32]))
+
+        w1_raw1 = load_raw(w1[:, BANK:H])
+        weights = held("tab_s", [P, 2, M], F32)
+        wa, wb = weights[:, 0, :], weights[:, 1, :]
+        nc.sync.dma_start(out=wa, in_=wga)
+        nc.sync.dma_start(out=wb, in_=wgb)
+        w3_raw1 = load_raw(w3[:, BANK:H])
+        w5_w = held("tab_w", [P, 2, N], I32)
+        nc.sync.dma_start(
+            out=w5_w[:], in_=w5_words.rearrange("a p c i -> a p (c i)").bitcast(I32).rearrange("a p c -> p a c")
+        )
+        w5_s = held("w3_dealt", [P, 2, N // 4], I32)
+        nc.gpsimd.memset(w5_s[:], 0)
+        load_scale_rows(nc.sync, w5_s, w5_scales.bitcast(I32).rearrange("a q c -> q a c"))
+        bias = held("w1_dealt", [P, N // P], F32)
+        with nc.allow_non_contiguous_dma(reason="one bias value a partition"):
+            nc.sync.dma_start(out=bias[:], in_=b.rearrange("(c p) -> p c", p=P))
+
+        h = [[held("h%d_%d" % (a, t), [P, S], F32) for t in range(PACK)] for a in range(2)]
+        xa = held("xa", [P, PACK, M], F32)
+        xb = held("xb", [P, PACK, M], F32)
+
+        def direct_products(t):
+            cols = slice(t * P, (t + 1) * P)
+            parts = []
+            for u in range(2):
+                mov = dict(rhs=v_w[u][:].bitcast(E4M3), rhs_scale=v_s[:, u * BANK : (u + 1) * BANK], start=True, stop=True)
+                h2 = psum.tile([P, BANK], F32, name="h2")
+                nc.tensor.matmul_mx(out=h2[:], lhsT=w2_dealt_w[:, cols].bitcast(E2M1), lhsT_scale=w2_dealt_s[:, cols], **mov)
+                h1 = psum.tile([P, BANK], F32, name="h1")
+                nc.tensor.matmul_mx(out=h1[:], lhsT=w1_q0[0][:, cols].bitcast(E4M3), lhsT_scale=w1_q0[1][:, cols], **mov)
+                h3 = psum.tile([P, BANK], F32, name="h3")
+                nc.tensor.matmul_mx(out=h3[:], lhsT=w3_q0[0][:, cols].bitcast(E4M3), lhsT_scale=w3_q0[1][:, cols], **mov)
+                h2_sb = ring.tile([P, BANK], F32, name="h2_sb")
+                nc.scalar.copy(out=h2_sb[:], in_=h2[:])
+                prod = ring.tile([P, BANK], F32, name="prod")
+                nc.vector.tensor_tensor(out=prod[:], in0=h1[:], in1=h2_sb[:], op=MULT)
+                parts.append((prod, h3))
+            return parts
+
+        def direct_sums(t, parts):
+            for u, (prod, h3) in enumerate(parts):
+                nc.vector.tensor_tensor(out=h[0][t][:, u * BANK : (u + 1) * BANK], in0=h3[:], in1=prod[:], op=ADD)
+
+        def pick(x, weight, lists, a, t):
+            nc.vector.tensor_tensor(out=x[:, t, :], in0=h[a][t][:].indirect(lists[:]), in1=weight, op=MULT)
+
+        turned = []
+
+        def turned_products(j, w1_q, w3_q):
+            u, cols = j // 4, slice((j % 4) * P, (j % 4 + 1) * P)
+            sta = dict(lhsT=v_w[u][:, cols].bitcast(E4M3), lhsT_scale=v_s[:, j * P : (j + 1) * P], start=True, stop=True)
+            h2 = psum.tile([P, BANK], F32, name="h2")
+            nc.tensor.matmul_mx(
+                out=h2[:], rhs=w2_w[:].bitcast(U16)[:, BANK:H].bitcast(E2M1), rhs_scale=w2_s[:].bitcast(U8)[:, BANK:H], **sta
+            )
+            h1 = psum.tile([P, BANK], F32, name="h1")
+            nc.tensor.matmul_mx(out=h1[:], rhs=w1_q[0][:].bitcast(E4M3), rhs_scale=w1_q[1][:], **sta)
+            h3 = psum.tile([P, BANK], F32, name="h3")
+            nc.tensor.matmul_mx(out=h3[:], rhs=w3_q[0][:].bitcast(E4M3), rhs_scale=w3_q[1][:], **sta)
+            h2_sb = ring.tile([P, PACK, P], F32, name="h2_sb")
+            nc.scalar.copy(out=h2_sb[:], in_=h2[:].rearrange("p (m t) -> p t m", t=PACK))
+            h3_sb = keep.tile([P, PACK, P], F32, name="h3_turned", bufs=6)
+            nc.scalar.copy(out=h3_sb[:], in_=h3[:].rearrange("p (m t) -> p t m", t=PACK))
+            prod = keep.tile([P, PACK, P], F32, name="prod_turned", bufs=6)
+            nc.vector.tensor_tensor(out=prod[:], in0=h1[:].rearrange("p (m t) -> p t m", t=PACK), in1=h2_sb[:], op=MULT)
+            turned.append((prod, h3_sb))
+
+        def turn_back(u):
+            for t in range(PACK):
+                bank = psum.tile([P, BANK], F32, name="turn")
+                for jj in range(4):
+                    prod, h3_sb = turned[4 * u + jj]
+                    dst = bank[:, jj * P : (jj + 1) * P]
+                    nc.tensor.matmul(out=dst, lhsT=h3_sb[:, t, :], rhs=ident[:], is_transpose=True, start=True, stop=False)
+                    nc.tensor.matmul(out=dst, lhsT=prod[:, t, :], rhs=ident[:], is_transpose=True, start=False, stop=True)
+                nc.scalar.copy(out=h[1][t][:, u * BANK : (u + 1) * BANK], in_=bank[:])
+
+        def join(op):
+            z = ring.tile([P, M, PACK], BF16, name="z", align_bytes=64)
+            nc.vector.tensor_tensor(
+                out=z[:].rearrange("p (c i) t -> p c t i", i=4),
+                in0=xa[:].rearrange("p t (c i) -> p c t i", i=4),
+                in1=xb[:].rearrange("p t (c i) -> p c t i", i=4),
+                op=op,
+            )
+            return z
+
+        direct_sums(0, direct_products(0))
+        for t in range(1, PACK):
+            parts = direct_products(t)
+            pick(xa, wa, idx2, 0, t - 1)
+            direct_sums(t, parts)
+            pick(xb, wb, idx3, 0, t - 1)
+            if t == 1:
+                w1_g1 = round_plain(w1_raw1)
+                w3_g1 = round_plain(w3_raw1)
+            if t == 2:
+                w1_q1 = quantise("w1_1", w1_g1)
+                w3_q1 = quantise("w3_1", w3_g1)
+        w4_raw = [load_raw(w4[a * PASS : (a + 1) * PASS, :]) for a in range(2)]
+        for j in range(4):
+            turned_products(j, w1_q1, w3_q1)
+        pick(xa, wa, idx2, 0, PACK - 1)
+        turn_back(0)
+        for j in range(4, 6):
+            turned_products(j, w1_q1, w3_q1)
+        pick(xb, wb, idx3, 0, PACK - 1)
+        for j in range(6, 8):
+            turned_products(j, w1_q1, w3_q1)
+        turn_back(1)
+
+        zm0 = join(MAX)
+        zp0 = join(MULT)
+        zm_q = [quantise("zm0", zm0)]
+        zp_q = [quantise("zp0", zp0)]
+        w4_g = [round_plain(raw) for raw in w4_raw]
+
+        y = [psum.tile([P, M], F32, name=name) for name in ("h1", "h1", "h3", "h3")]
+
+        def score_pass(a, z_q, from_w4, start, stop):
+            for n in range(N // P):
+                cols = slice(n * P, (n + 1) * P)
+                if from_w4:
+                    codes, scales = w4_q[a][0][:, cols], w4_q[a][1][:, cols]
+                else:
+                    codes, scales = w5_w[:, a, cols], w5_s[:, a, :].bitcast(U8)[:, cols]
+                nc.tensor.matmul_mx(
+                    out=y[n][:], lhsT=codes.bitcast(E4M3), lhsT_scale=scales,
+                    rhs=z_q[0][:].bitcast(E4M3), rhs_scale=z_q[1][:], start=start, stop=stop,
+                )
+
+        w4_q = []
+        for t in range(PACK):
+            pick(xa, wa, idx2, 1, t)
+            pick(xb, wb, idx3, 1, t)
+            if t in (1, 2):
+                w4_q.append(quantise("w4_%d" % (t - 1), w4_g[t - 1]))
+        score_pass(0, zp_q[0], False, True, False)
+        score_pass(0, zm_q[0], True, False, False)
+        zm_q.append(quantise("zm1", join(MAX)))
+        score_pass(1, zm_q[1], True, False, False)
+        zp_q.append(quantise("zp1", join(MULT)))
+        score_pass(1, zp_q[1], False, False, True)
+
+        for n in range(N // P):
+            res = raws.tile([P, M], F32, name="res", bufs=4)
+            nc.scalar.activation(out=res[:], in_=y[n][:], func=GELU, bias=bias[:, n : n + 1])
+            nc.sync.dma_start(out=out[n * P : (n + 1) * P, :], in_=res[:])

@@ -32,15 +32,15 @@ def tile_list_mycorrhiza_transfer_score_kernel(
     with ExitStack() as ctx:
         keep = ctx.enter_context(tc.tile_pool(name="keep", bufs=1))
         ring = ctx.enter_context(tc.tile_pool(name="ring", bufs=2))
-        raws = ctx.enter_context(tc.tile_pool(name="raws", bufs=2))
-        psum = ctx.enter_context(tc.psum_pool(name="psum", bufs=2))
+        raws = ctx.enter_context(tc.tile_pool(name="raws", bufs=4))
+        psum = ctx.enter_context(tc.psum_pool(name="psum", bufs=4))
 
         def held(name, shape, dtype):
             return keep.tile(shape, dtype, name=name, align_bytes=64)
 
-        def load_scale_rows(queue, plane, rows):
+        def load_scale_rows(plane, rows):
             for q in range(4):
-                queue.dma_start(out=plane[32 * q : 32 * q + 4], in_=rows[4 * q : 4 * q + 4])
+                nc.sync.dma_start(out=plane[32 * q : 32 * q + 4], in_=rows[4 * q : 4 * q + 4])
 
         def load_raw(rows):
             raw = raws.tile([P, PACK, BANK], F32, name="raw")
@@ -55,8 +55,8 @@ def tile_list_mycorrhiza_transfer_score_kernel(
             )
             return grouped
 
-        def round_dealt(raw, name):
-            grouped = held(name, [P, BANK, PACK], BF16)
+        def round_dealt(raw):
+            grouped = ring.tile([P, BANK, PACK], BF16, name="grouped", align_bytes=64)
             nc.scalar.copy(
                 out=grouped[:].rearrange("p (t m) j -> p m j t", t=PACK),
                 in_=raw[:].rearrange("p j (m t) -> p m j t", t=PACK),
@@ -64,8 +64,9 @@ def tile_list_mycorrhiza_transfer_score_kernel(
             return grouped
 
         def quantise(name, grouped):
-            codes = held(name + "_codes", [P, BANK], U32)
-            scales = held(name + "_scales", [P, BANK], U8)
+            width = grouped.shape[1]
+            codes = held(name + "_codes", [P, width], U32)
+            scales = held(name + "_scales", [P, width], U8)
             nc.vector.quantize_mx(
                 out=codes[:].bitcast(E4M3), scales=scales[:], in_=grouped[:].rearrange("p c j -> p (c j)")
             )
@@ -78,57 +79,56 @@ def tile_list_mycorrhiza_transfer_score_kernel(
         tab_s = held("tab_s", [P, T // 4], I32)
         w2_w = held("w2_w", [P, 2 * H // 4], I32)
         w2_s = held("w2_s", [P, H // 4], I32)
+        w5_w = held("w5_w", [P, 2, N], I32)
+        w5_s = held("w5_s", [P, 2, N // 4], I32)
+        wa = held("wa", [P, M], F32)
+        wb = held("wb", [P, M], F32)
+        bias = held("bias", [P, N // P], F32)
         ident = held("ident", [P, P], F32)
 
         nc.vector.memset(tab_s[:], 0)
         nc.gpsimd.memset(w2_s[:], 0)
-        load_scale_rows(nc.gpsimd, w2_s, w2_scales[0].bitcast(I32))
+        nc.gpsimd.memset(w5_s[:], 0)
         make_identity(nc, ident[:])
+        w1_raw0 = load_raw(w1[:, 0:BANK])
+        load_scale_rows(tab_s, tab_scales[0].bitcast(I32))
         nc.sync.dma_start(out=idx[:], in_=offs)
+        w3_raw0 = load_raw(w3[:, 0:BANK])
+        nc.sync.dma_start(out=w2_w[:], in_=w2_words[0].bitcast(I32))
+        load_scale_rows(w2_s, w2_scales[0].bitcast(I32))
+        nc.sync.dma_start(out=tab_w[:], in_=tab_words[0].rearrange("p t i -> p (t i)").bitcast(I32))
         nc.sync.dma_start(out=idx2[:], in_=offs2)
         nc.sync.dma_start(out=idx3[:], in_=offs3)
-        nc.sync.dma_start(out=w2_w[:], in_=w2_words[0].bitcast(I32))
-        w1_raw0 = load_raw(w1[:, 0:BANK])
-        w3_raw0 = load_raw(w3[:, 0:BANK])
-        nc.sync.dma_start(out=tab_w[:], in_=tab_words[0].rearrange("p t i -> p (t i)").bitcast(I32))
-        load_scale_rows(nc.scalar, tab_s, tab_scales[0].bitcast(I32))
+        nc.sync.dma_start(out=wa[:], in_=wga)
+        nc.sync.dma_start(out=wb[:], in_=wgb)
+        w1_raw1 = load_raw(w1[:, BANK:H])
+        w3_raw1 = load_raw(w3[:, BANK:H])
+        nc.sync.dma_start(
+            out=w5_w[:], in_=w5_words.rearrange("a p c i -> a p (c i)").bitcast(I32).rearrange("a p c -> p a c")
+        )
+        load_scale_rows(w5_s, w5_scales.bitcast(I32).rearrange("a q c -> q a c"))
+        with nc.allow_non_contiguous_dma(reason="one bias value a partition"):
+            nc.sync.dma_start(out=bias[:], in_=b.rearrange("(c p) -> p c", p=P))
 
         v_s = held("v_s", [P, S], U8)
         nc.vector.tensor_copy(out=v_s[:], in_=tab_s[:].bitcast(U8).indirect(idx[:]))
 
-        w2_dealt_w = held("w2_dealt_w", [P, BANK], U16)
-        w2_dealt_s = held("w2_dealt_s", [P, BANK], U8)
+        w2_dealt_w = held("w2_dealt_w", [P, 2, BANK], U16)
+        w2_dealt_s = held("w2_dealt_s", [P, 2, BANK], U8)
         nc.vector.tensor_copy(
-            out=w2_dealt_w[:].rearrange("p (t m) -> p t m", t=PACK),
-            in_=w2_w[:].bitcast(U16)[:, 0:BANK].rearrange("p (m t) -> p t m", t=PACK),
+            out=w2_dealt_w[:].rearrange("p a (t m) -> p a t m", t=PACK),
+            in_=w2_w[:].bitcast(U16).rearrange("p (a m t) -> p a t m", a=2, t=PACK),
         )
         nc.vector.tensor_copy(
-            out=w2_dealt_s[:].rearrange("p (t m) -> p t m", t=PACK),
-            in_=w2_s[:].bitcast(U8)[:, 0:BANK].rearrange("p (m t) -> p t m", t=PACK),
+            out=w2_dealt_s[:].rearrange("p a (t m) -> p a t m", t=PACK),
+            in_=w2_s[:].bitcast(U8).rearrange("p (a m t) -> p a t m", a=2, t=PACK),
         )
-        w1_q0 = quantise("w1_0", round_dealt(w1_raw0, "w1_dealt"))
-        w3_q0 = quantise("w3_0", round_dealt(w3_raw0, "w3_dealt"))
+        w1_q0 = quantise("w1_0", round_dealt(w1_raw0))
+        w3_q0 = quantise("w3_0", round_dealt(w3_raw0))
 
         v_w = [held("v_w%d" % u, [P, BANK], U32) for u in range(2)]
         for u in range(2):
             nc.vector.tensor_copy(out=v_w[u][:], in_=tab_w[:].bitcast(U32).indirect(idx[:, 32 * u : 32 * u + 32]))
-
-        w1_raw1 = load_raw(w1[:, BANK:H])
-        weights = held("tab_s", [P, 2, M], F32)
-        wa, wb = weights[:, 0, :], weights[:, 1, :]
-        nc.sync.dma_start(out=wa, in_=wga)
-        nc.sync.dma_start(out=wb, in_=wgb)
-        w3_raw1 = load_raw(w3[:, BANK:H])
-        w5_w = held("tab_w", [P, 2, N], I32)
-        nc.sync.dma_start(
-            out=w5_w[:], in_=w5_words.rearrange("a p c i -> a p (c i)").bitcast(I32).rearrange("a p c -> p a c")
-        )
-        w5_s = held("w3_dealt", [P, 2, N // 4], I32)
-        nc.gpsimd.memset(w5_s[:], 0)
-        load_scale_rows(nc.sync, w5_s, w5_scales.bitcast(I32).rearrange("a q c -> q a c"))
-        bias = held("w1_dealt", [P, N // P], F32)
-        with nc.allow_non_contiguous_dma(reason="one bias value a partition"):
-            nc.sync.dma_start(out=bias[:], in_=b.rearrange("(c p) -> p c", p=P))
 
         h = [[held("h%d_%d" % (a, t), [P, S], F32) for t in range(PACK)] for a in range(2)]
         xa = held("xa", [P, PACK, M], F32)
@@ -139,13 +139,13 @@ def tile_list_mycorrhiza_transfer_score_kernel(
             parts = []
             for u in range(2):
                 mov = dict(rhs=v_w[u][:].bitcast(E4M3), rhs_scale=v_s[:, u * BANK : (u + 1) * BANK], start=True, stop=True)
-                h2 = psum.tile([P, BANK], F32, name="h2")
-                nc.tensor.matmul_mx(out=h2[:], lhsT=w2_dealt_w[:, cols].bitcast(E2M1), lhsT_scale=w2_dealt_s[:, cols], **mov)
-                h1 = psum.tile([P, BANK], F32, name="h1")
+                h2 = psum.tile([P, BANK], F32, name="by_scalar")
+                nc.tensor.matmul_mx(out=h2[:], lhsT=w2_dealt_w[:, 0, cols].bitcast(E2M1), lhsT_scale=w2_dealt_s[:, 0, cols], **mov)
+                h1 = psum.tile([P, BANK], F32, name="by_vector")
                 nc.tensor.matmul_mx(out=h1[:], lhsT=w1_q0[0][:, cols].bitcast(E4M3), lhsT_scale=w1_q0[1][:, cols], **mov)
-                h3 = psum.tile([P, BANK], F32, name="h3")
+                h3 = psum.tile([P, BANK], F32, name="by_vector")
                 nc.tensor.matmul_mx(out=h3[:], lhsT=w3_q0[0][:, cols].bitcast(E4M3), lhsT_scale=w3_q0[1][:, cols], **mov)
-                h2_sb = ring.tile([P, BANK], F32, name="h2_sb")
+                h2_sb = ring.tile([P, BANK], F32, name="h2_sb", bufs=4)
                 nc.scalar.copy(out=h2_sb[:], in_=h2[:])
                 prod = ring.tile([P, BANK], F32, name="prod")
                 nc.vector.tensor_tensor(out=prod[:], in0=h1[:], in1=h2_sb[:], op=MULT)
@@ -157,107 +157,137 @@ def tile_list_mycorrhiza_transfer_score_kernel(
                 nc.vector.tensor_tensor(out=h[0][t][:, u * BANK : (u + 1) * BANK], in0=h3[:], in1=prod[:], op=ADD)
 
         def pick(x, weight, lists, a, t):
-            nc.vector.tensor_tensor(out=x[:, t, :], in0=h[a][t][:].indirect(lists[:]), in1=weight, op=MULT)
+            nc.vector.tensor_tensor(out=x[:, t, :], in0=h[a][t][:].indirect(lists[:]), in1=weight[:], op=MULT)
 
-        turned = []
+        def turned_products(a, first, r, w1_q, w3_q, h2_sb=None):
+            cols = slice(first * P, BANK)
+            width = BANK - first * P
+            per_bank = BANK // width
+            h2 = psum.tile([P, per_bank, width], F32, name="by_scalar")
+            h1 = psum.tile([P, per_bank, width], F32, name="by_vector")
+            h3 = psum.tile([P, per_bank, width], F32, name="by_scalar")
+            for bank, codes, scales in (
+                (h2, w2_dealt_w[:, a, cols].bitcast(E2M1), w2_dealt_s[:, a, cols]),
+                (h1, w1_q[0][:, cols].bitcast(E4M3), w1_q[1][:, cols]),
+                (h3, w3_q[0][:, cols].bitcast(E4M3), w3_q[1][:, cols]),
+            ):
+                for jj in range(per_bank):
+                    j = r * per_bank + jj
+                    nc.tensor.matmul_mx(
+                        out=bank[:, jj, :], lhsT=v_w[j // 4][:, (j % 4) * P : (j % 4 + 1) * P].bitcast(E4M3),
+                        lhsT_scale=v_s[:, j * P : (j + 1) * P], rhs=codes, rhs_scale=scales, start=True, stop=True,
+                    )
+            if h2_sb is None:
+                h2_sb = ring.tile([P, per_bank, width], F32, name="h2_sb", bufs=4)
+            nc.scalar.copy(out=h2_sb[:], in_=h2[:])
+            h3_sb = keep.tile([P, per_bank, width], F32, name="h3_turned", bufs=8)
+            nc.scalar.copy(out=h3_sb[:], in_=h3[:])
+            prod = keep.tile([P, per_bank, width], F32, name="prod_turned", bufs=8)
+            nc.vector.tensor_tensor(out=prod[:], in0=h1[:], in1=h2_sb[:], op=MULT)
+            return [(prod[:, jj, :], h3_sb[:, jj, :]) for jj in range(per_bank)]
 
-        def turned_products(j, w1_q, w3_q):
-            u, cols = j // 4, slice((j % 4) * P, (j % 4 + 1) * P)
-            sta = dict(lhsT=v_w[u][:, cols].bitcast(E4M3), lhsT_scale=v_s[:, j * P : (j + 1) * P], start=True, stop=True)
-            h2 = psum.tile([P, BANK], F32, name="h2")
-            nc.tensor.matmul_mx(
-                out=h2[:], rhs=w2_w[:].bitcast(U16)[:, BANK:H].bitcast(E2M1), rhs_scale=w2_s[:].bitcast(U8)[:, BANK:H], **sta
-            )
-            h1 = psum.tile([P, BANK], F32, name="h1")
-            nc.tensor.matmul_mx(out=h1[:], rhs=w1_q[0][:].bitcast(E4M3), rhs_scale=w1_q[1][:], **sta)
-            h3 = psum.tile([P, BANK], F32, name="h3")
-            nc.tensor.matmul_mx(out=h3[:], rhs=w3_q[0][:].bitcast(E4M3), rhs_scale=w3_q[1][:], **sta)
-            h2_sb = ring.tile([P, PACK, P], F32, name="h2_sb")
-            nc.scalar.copy(out=h2_sb[:], in_=h2[:].rearrange("p (m t) -> p t m", t=PACK))
-            h3_sb = keep.tile([P, PACK, P], F32, name="h3_turned", bufs=6)
-            nc.scalar.copy(out=h3_sb[:], in_=h3[:].rearrange("p (m t) -> p t m", t=PACK))
-            prod = keep.tile([P, PACK, P], F32, name="prod_turned", bufs=6)
-            nc.vector.tensor_tensor(out=prod[:], in0=h1[:].rearrange("p (m t) -> p t m", t=PACK), in1=h2_sb[:], op=MULT)
-            turned.append((prod, h3_sb))
+        def turn_back(a, first, t, u, turned):
+            cols = slice((t - first) * P, (t - first + 1) * P)
+            bank = psum.tile([P, BANK], F32, name="by_scalar")
+            for jj in range(4):
+                prod, h3_sb = turned[4 * u + jj]
+                dst = bank[:, jj * P : (jj + 1) * P]
+                nc.tensor.matmul(out=dst, lhsT=h3_sb[:, cols], rhs=ident[:], is_transpose=True, start=True, stop=False)
+                nc.tensor.matmul(out=dst, lhsT=prod[:, cols], rhs=ident[:], is_transpose=True, start=False, stop=True)
+            nc.scalar.copy(out=h[a][t][:, u * BANK : (u + 1) * BANK], in_=bank[:])
 
-        def turn_back(u):
-            for t in range(PACK):
-                bank = psum.tile([P, BANK], F32, name="turn")
-                for jj in range(4):
-                    prod, h3_sb = turned[4 * u + jj]
-                    dst = bank[:, jj * P : (jj + 1) * P]
-                    nc.tensor.matmul(out=dst, lhsT=h3_sb[:, t, :], rhs=ident[:], is_transpose=True, start=True, stop=False)
-                    nc.tensor.matmul(out=dst, lhsT=prod[:, t, :], rhs=ident[:], is_transpose=True, start=False, stop=True)
-                nc.scalar.copy(out=h[1][t][:, u * BANK : (u + 1) * BANK], in_=bank[:])
-
-        def join(op):
-            z = ring.tile([P, M, PACK], BF16, name="z", align_bytes=64)
+        def join(op, cols, name):
+            z = held(name, [P, cols.stop - cols.start, PACK], BF16)
             nc.vector.tensor_tensor(
                 out=z[:].rearrange("p (c i) t -> p c t i", i=4),
-                in0=xa[:].rearrange("p t (c i) -> p c t i", i=4),
-                in1=xb[:].rearrange("p t (c i) -> p c t i", i=4),
+                in0=xa[:, :, cols].rearrange("p t (c i) -> p c t i", i=4),
+                in1=xb[:, :, cols].rearrange("p t (c i) -> p c t i", i=4),
                 op=op,
             )
             return z
 
-        direct_sums(0, direct_products(0))
-        for t in range(1, PACK):
-            parts = direct_products(t)
-            pick(xa, wa, idx2, 0, t - 1)
-            direct_sums(t, parts)
-            pick(xb, wb, idx3, 0, t - 1)
-            if t == 1:
-                w1_g1 = round_plain(w1_raw1)
-                w3_g1 = round_plain(w3_raw1)
-            if t == 2:
-                w1_q1 = quantise("w1_1", w1_g1)
-                w3_q1 = quantise("w3_1", w3_g1)
+        every = slice(0, M)
+        halves = [slice(0, M // 2), slice(M // 2, M)]
         w4_raw = [load_raw(w4[a * PASS : (a + 1) * PASS, :]) for a in range(2)]
-        for j in range(4):
-            turned_products(j, w1_q1, w3_q1)
-        pick(xa, wa, idx2, 0, PACK - 1)
-        turn_back(0)
-        for j in range(4, 6):
-            turned_products(j, w1_q1, w3_q1)
-        pick(xb, wb, idx3, 0, PACK - 1)
-        for j in range(6, 8):
-            turned_products(j, w1_q1, w3_q1)
-        turn_back(1)
-
-        zm0 = join(MAX)
-        zp0 = join(MULT)
-        zm_q = [quantise("zm0", zm0)]
-        zp_q = [quantise("zp0", zp0)]
+        direct_sums(0, direct_products(0))
+        parts = direct_products(1)
+        low = turned_products(0, 2, 0, w1_q0, w3_q0)
+        pick(xa, wa, idx2, 0, 0)
+        direct_sums(1, parts)
+        low += turned_products(0, 2, 1, w1_q0, w3_q0)
+        pick(xb, wb, idx3, 0, 0)
+        low += turned_products(0, 2, 2, w1_q0, w3_q0)
+        turn_back(0, 2, 2, 0, low)
+        low += turned_products(0, 2, 3, w1_q0, w3_q0)
+        turn_back(0, 2, 2, 1, low)
+        w1_g1 = round_dealt(w1_raw1)
+        turn_back(0, 2, 3, 0, low)
+        turn_back(0, 2, 3, 1, low)
+        w3_g1 = round_dealt(w3_raw1)
+        pick(xa, wa, idx2, 0, 1)
+        pick(xb, wb, idx3, 0, 1)
+        w1_q1 = quantise("w1_1", w1_g1)
+        pick(xa, wa, idx2, 0, 2)
+        w3_q1 = quantise("w3_1", w3_g1)
+        pick(xb, wb, idx3, 0, 2)
+        high = turned_products(1, 0, 0, w1_q1, w3_q1)
+        pick(xa, wa, idx2, 0, 3)
+        high += turned_products(1, 0, 1, w1_q1, w3_q1)
+        pick(xb, wb, idx3, 0, 3)
+        high += turned_products(1, 0, 2, w1_q1, w3_q1)
+        high += turned_products(1, 0, 3, w1_q1, w3_q1, held("zm", [P, 1, BANK], F32))
+        zm0 = join(MAX, every, "zm")
+        for t in range(2):
+            high += turned_products(1, 0, 4 + t, w1_q1, w3_q1)
+            turn_back(1, 0, t, 0, high)
+        zm0_q = quantise("zm0", zm0)
+        high += turned_products(1, 0, 6, w1_q1, w3_q1)
+        high += turned_products(1, 0, 7, w1_q1, w3_q1, held("zp", [P, 1, BANK], F32))
+        turn_back(1, 0, 0, 1, high)
+        turn_back(1, 0, 1, 1, high)
+        for t in range(2, 4):
+            for u in range(2):
+                turn_back(1, 0, t, u, high)
+        zp0 = join(MULT, every, "zp")
         w4_g = [round_plain(raw) for raw in w4_raw]
 
-        y = [psum.tile([P, M], F32, name=name) for name in ("h1", "h1", "h3", "h3")]
+        y = [[psum.tile([P, M // 2], F32, name=name) for n in range(N // P)] for name in ("by_vector", "by_scalar")]
 
-        def score_pass(a, z_q, from_w4, start, stop):
+        def score_pass(u, w_codes, w_scales, z_q, z_cols, start, stop):
             for n in range(N // P):
                 cols = slice(n * P, (n + 1) * P)
-                if from_w4:
-                    codes, scales = w4_q[a][0][:, cols], w4_q[a][1][:, cols]
-                else:
-                    codes, scales = w5_w[:, a, cols], w5_s[:, a, :].bitcast(U8)[:, cols]
                 nc.tensor.matmul_mx(
-                    out=y[n][:], lhsT=codes.bitcast(E4M3), lhsT_scale=scales,
-                    rhs=z_q[0][:].bitcast(E4M3), rhs_scale=z_q[1][:], start=start, stop=stop,
+                    out=y[u][n][:], lhsT=w_codes[:, cols].bitcast(E4M3), lhsT_scale=w_scales[:, cols],
+                    rhs=z_q[0][:, z_cols].bitcast(E4M3), rhs_scale=z_q[1][:, z_cols], start=start, stop=stop,
                 )
 
-        w4_q = []
-        for t in range(PACK):
+        def finish(u):
+            for n in range(N // P):
+                res = raws.tile([P, M // 2], F32, name="res", bufs=8)
+                nc.scalar.activation(out=res[:], in_=y[u][n][:], func=GELU, bias=bias[:, n : n + 1])
+                nc.sync.dma_start(out=out[n * P : (n + 1) * P, halves[u]], in_=res[:])
+
+        w5_q = [(w5_w[:, a, :], w5_s[:, a, :].bitcast(U8)) for a in range(2)]
+        for t in range(PACK - 1):
             pick(xa, wa, idx2, 1, t)
             pick(xb, wb, idx3, 1, t)
-            if t in (1, 2):
-                w4_q.append(quantise("w4_%d" % (t - 1), w4_g[t - 1]))
-        score_pass(0, zp_q[0], False, True, False)
-        score_pass(0, zm_q[0], True, False, False)
-        zm_q.append(quantise("zm1", join(MAX)))
-        score_pass(1, zm_q[1], True, False, False)
-        zp_q.append(quantise("zp1", join(MULT)))
-        score_pass(1, zp_q[1], False, False, True)
-
-        for n in range(N // P):
-            res = raws.tile([P, M], F32, name="res", bufs=4)
-            nc.scalar.activation(out=res[:], in_=y[n][:], func=GELU, bias=bias[:, n : n + 1])
-            nc.sync.dma_start(out=out[n * P : (n + 1) * P, :], in_=res[:])
+        w4_q1 = quantise("w4_1", w4_g[1])
+        pick(xa, wa, idx2, 1, PACK - 1)
+        zp0_q = quantise("zp0", zp0)
+        pick(xb, wb, idx3, 1, PACK - 1)
+        w4_q0 = quantise("w4_0", w4_g[0])
+        for u in range(2):
+            score_pass(u, *w5_q[0], zp0_q, halves[u], True, False)
+        for u in range(2):
+            score_pass(u, *w4_q0, zm0_q, halves[u], False, False)
+        zm1 = join(MAX, every, "zm")
+        zp1 = join(MULT, halves[0], "zp")
+        zm1_q = quantise("zm1", zm1)
+        zp1_q = quantise("zp1a", zp1)
+        score_pass(0, *w4_q1, zm1_q, halves[0], False, False)
+        score_pass(0, *w5_q[1], zp1_q, halves[0], False, True)
+        finish(0)
+        score_pass(1, *w4_q1, zm1_q, halves[1], False, False)
+        zp1_q = quantise("zp1b", join(MULT, halves[1], "zp_last"))
+        score_pass(1, *w5_q[1], zp1_q, halves[0], False, True)
+        finish(1)

@@ -38,9 +38,9 @@ def tile_list_mycorrhiza_transfer_score_kernel(
         def held(name, shape, dtype):
             return keep.tile(shape, dtype, name=name, align_bytes=64)
 
-        def load_scale_rows(plane, rows):
+        def load_scale_rows(queue, plane, rows):
             for q in range(4):
-                nc.sync.dma_start(out=plane[32 * q : 32 * q + 4], in_=rows[4 * q : 4 * q + 4])
+                queue.dma_start(out=plane[32 * q : 32 * q + 4], in_=rows[4 * q : 4 * q + 4])
 
         def load_raw(rows):
             raw = raws.tile([P, PACK, BANK], F32, name="raw")
@@ -55,17 +55,17 @@ def tile_list_mycorrhiza_transfer_score_kernel(
             )
             return grouped
 
-        def round_dealt(raw):
-            grouped = ring.tile([P, BANK, PACK], BF16, name="grouped", align_bytes=64)
+        def round_dealt(raw, pair):
+            grouped = ring.tile([P, 2 * P, PACK], BF16, name="dealt", bufs=4, align_bytes=64)
             nc.scalar.copy(
-                out=grouped[:].rearrange("p (t m) j -> p m j t", t=PACK),
-                in_=raw[:].rearrange("p j (m t) -> p m j t", t=PACK),
+                out=grouped[:].rearrange("p (t m) j -> p m j t", t=2),
+                in_=raw[:].rearrange("p j (m t) -> p m j t", t=PACK)[:, :, :, 2 * pair : 2 * pair + 2],
             )
             return grouped
 
-        def quantise(name, grouped):
+        def quantise(name, grouped, codes_name=None):
             width = grouped.shape[1]
-            codes = held(name + "_codes", [P, width], U32)
+            codes = held(codes_name or name + "_codes", [P, width], U32)
             scales = held(name + "_scales", [P, width], U8)
             nc.vector.quantize_mx(
                 out=codes[:].bitcast(E4M3), scales=scales[:], in_=grouped[:].rearrange("p c j -> p (c j)")
@@ -91,11 +91,11 @@ def tile_list_mycorrhiza_transfer_score_kernel(
         nc.gpsimd.memset(w5_s[:], 0)
         make_identity(nc, ident[:])
         w1_raw0 = load_raw(w1[:, 0:BANK])
-        load_scale_rows(tab_s, tab_scales[0].bitcast(I32))
+        load_scale_rows(nc.sync, tab_s, tab_scales[0].bitcast(I32))
         nc.sync.dma_start(out=idx[:], in_=offs)
         w3_raw0 = load_raw(w3[:, 0:BANK])
         nc.sync.dma_start(out=w2_w[:], in_=w2_words[0].bitcast(I32))
-        load_scale_rows(w2_s, w2_scales[0].bitcast(I32))
+        load_scale_rows(nc.sync, w2_s, w2_scales[0].bitcast(I32))
         nc.sync.dma_start(out=tab_w[:], in_=tab_words[0].rearrange("p t i -> p (t i)").bitcast(I32))
         nc.sync.dma_start(out=idx2[:], in_=offs2)
         nc.sync.dma_start(out=idx3[:], in_=offs3)
@@ -106,7 +106,7 @@ def tile_list_mycorrhiza_transfer_score_kernel(
         nc.sync.dma_start(
             out=w5_w[:], in_=w5_words.rearrange("a p c i -> a p (c i)").bitcast(I32).rearrange("a p c -> p a c")
         )
-        load_scale_rows(w5_s, w5_scales.bitcast(I32).rearrange("a q c -> q a c"))
+        load_scale_rows(nc.sync, w5_s, w5_scales.bitcast(I32).rearrange("a q c -> q a c"))
         with nc.allow_non_contiguous_dma(reason="one bias value a partition"):
             nc.sync.dma_start(out=bias[:], in_=b.rearrange("(c p) -> p c", p=P))
 
@@ -123,8 +123,8 @@ def tile_list_mycorrhiza_transfer_score_kernel(
             out=w2_dealt_s[:].rearrange("p a (t m) -> p a t m", t=PACK),
             in_=w2_s[:].bitcast(U8).rearrange("p (a m t) -> p a t m", a=2, t=PACK),
         )
-        w1_q0 = quantise("w1_0", round_dealt(w1_raw0))
-        w3_q0 = quantise("w3_0", round_dealt(w3_raw0))
+        w1_q = {(0, pair): quantise("w1_0%d" % pair, round_dealt(w1_raw0, pair)) for pair in range(2)}
+        w3_q = {(0, pair): quantise("w3_0%d" % pair, round_dealt(w3_raw0, pair)) for pair in range(2)}
 
         v_w = [held("v_w%d" % u, [P, BANK], U32) for u in range(2)]
         for u in range(2):
@@ -134,60 +134,63 @@ def tile_list_mycorrhiza_transfer_score_kernel(
         xa = held("xa", [P, PACK, M], F32)
         xb = held("xb", [P, PACK, M], F32)
 
-        def direct_products(t):
-            cols = slice(t * P, (t + 1) * P)
-            parts = []
-            for u in range(2):
-                mov = dict(rhs=v_w[u][:].bitcast(E4M3), rhs_scale=v_s[:, u * BANK : (u + 1) * BANK], start=True, stop=True)
-                h2 = psum.tile([P, BANK], F32, name="by_scalar")
-                nc.tensor.matmul_mx(out=h2[:], lhsT=w2_dealt_w[:, 0, cols].bitcast(E2M1), lhsT_scale=w2_dealt_s[:, 0, cols], **mov)
-                h1 = psum.tile([P, BANK], F32, name="by_vector")
-                nc.tensor.matmul_mx(out=h1[:], lhsT=w1_q0[0][:, cols].bitcast(E4M3), lhsT_scale=w1_q0[1][:, cols], **mov)
-                h3 = psum.tile([P, BANK], F32, name="by_vector")
-                nc.tensor.matmul_mx(out=h3[:], lhsT=w3_q0[0][:, cols].bitcast(E4M3), lhsT_scale=w3_q0[1][:, cols], **mov)
-                h2_sb = ring.tile([P, BANK], F32, name="h2_sb", bufs=4)
-                nc.scalar.copy(out=h2_sb[:], in_=h2[:])
-                prod = ring.tile([P, BANK], F32, name="prod")
-                nc.vector.tensor_tensor(out=prod[:], in0=h1[:], in1=h2_sb[:], op=MULT)
-                parts.append((prod, h3))
-            return parts
+        def moving_table(u):
+            return dict(rhs=v_w[u][:].bitcast(E4M3), rhs_scale=v_s[:, u * BANK : (u + 1) * BANK], start=True, stop=True)
 
-        def direct_sums(t, parts):
-            for u, (prod, h3) in enumerate(parts):
-                nc.vector.tensor_tensor(out=h[0][t][:, u * BANK : (u + 1) * BANK], in0=h3[:], in1=prod[:], op=ADD)
+        def direct_product(t, u):
+            cols = slice(t * P, (t + 1) * P)
+            h2 = psum.tile([P, BANK], F32, name="by_scalar")
+            nc.tensor.matmul_mx(
+                out=h2[:], lhsT=w2_dealt_w[:, 0, cols].bitcast(E2M1), lhsT_scale=w2_dealt_s[:, 0, cols], **moving_table(u)
+            )
+            h1 = psum.tile([P, BANK], F32, name="by_vector")
+            codes, scales = w1_q[0, 0]
+            nc.tensor.matmul_mx(out=h1[:], lhsT=codes[:, cols].bitcast(E4M3), lhsT_scale=scales[:, cols], **moving_table(u))
+            h2_sb = ring.tile([P, BANK], F32, name="h2_sb", bufs=4)
+            nc.scalar.copy(out=h2_sb[:], in_=h2[:])
+            prod = ring.tile([P, BANK], F32, name="prod", bufs=4)
+            nc.vector.tensor_tensor(out=prod[:], in0=h1[:], in1=h2_sb[:], op=MULT)
+            return prod
+
+        def direct_sum(t, u, prod):
+            cols = slice(t * P, (t + 1) * P)
+            h3 = psum.tile([P, BANK], F32, name="by_vector")
+            codes, scales = w3_q[0, 0]
+            nc.tensor.matmul_mx(out=h3[:], lhsT=codes[:, cols].bitcast(E4M3), lhsT_scale=scales[:, cols], **moving_table(u))
+            nc.vector.tensor_tensor(out=h[0][t][:, u * BANK : (u + 1) * BANK], in0=h3[:], in1=prod[:], op=ADD)
 
         def pick(x, weight, lists, a, t):
             nc.vector.tensor_tensor(out=x[:, t, :], in0=h[a][t][:].indirect(lists[:]), in1=weight[:], op=MULT)
 
-        def turned_products(a, first, r, w1_q, w3_q, h2_sb=None):
-            cols = slice(first * P, BANK)
-            width = BANK - first * P
-            per_bank = BANK // width
-            h2 = psum.tile([P, per_bank, width], F32, name="by_scalar")
-            h1 = psum.tile([P, per_bank, width], F32, name="by_vector")
-            h3 = psum.tile([P, per_bank, width], F32, name="by_scalar")
+        def turned_products(a, pair, r, h2_sb=None):
+            cols = slice(pair * 2 * P, (pair + 1) * 2 * P)
+            h2 = psum.tile([P, 2, 2 * P], F32, name="by_scalar")
+            h1 = psum.tile([P, 2, 2 * P], F32, name="by_vector")
+            h3 = psum.tile([P, 2, 2 * P], F32, name="by_scalar")
             for bank, codes, scales in (
                 (h2, w2_dealt_w[:, a, cols].bitcast(E2M1), w2_dealt_s[:, a, cols]),
-                (h1, w1_q[0][:, cols].bitcast(E4M3), w1_q[1][:, cols]),
-                (h3, w3_q[0][:, cols].bitcast(E4M3), w3_q[1][:, cols]),
+                (h1, w1_q[a, pair][0][:].bitcast(E4M3), w1_q[a, pair][1][:]),
+                (h3, w3_q[a, pair][0][:].bitcast(E4M3), w3_q[a, pair][1][:]),
             ):
-                for jj in range(per_bank):
-                    j = r * per_bank + jj
+                for jj in range(2):
+                    j = 2 * r + jj
                     nc.tensor.matmul_mx(
                         out=bank[:, jj, :], lhsT=v_w[j // 4][:, (j % 4) * P : (j % 4 + 1) * P].bitcast(E4M3),
                         lhsT_scale=v_s[:, j * P : (j + 1) * P], rhs=codes, rhs_scale=scales, start=True, stop=True,
                     )
             if h2_sb is None:
-                h2_sb = ring.tile([P, per_bank, width], F32, name="h2_sb", bufs=4)
-            nc.scalar.copy(out=h2_sb[:], in_=h2[:])
-            h3_sb = keep.tile([P, per_bank, width], F32, name="h3_turned", bufs=8)
+                h2_sb = ring.tile([P, BANK], F32, name="h2_sb", bufs=4)[:]
+            nc.scalar.copy(out=h2_sb, in_=h2[:].rearrange("p j c -> p (j c)"))
+            h3_sb = keep.tile([P, 2, 2 * P], F32, name="h3_turned", bufs=8)
             nc.scalar.copy(out=h3_sb[:], in_=h3[:])
-            prod = keep.tile([P, per_bank, width], F32, name="prod_turned", bufs=8)
-            nc.vector.tensor_tensor(out=prod[:], in0=h1[:], in1=h2_sb[:], op=MULT)
-            return [(prod[:, jj, :], h3_sb[:, jj, :]) for jj in range(per_bank)]
+            prod = keep.tile([P, 2, 2 * P], F32, name="prod_turned", bufs=8)
+            nc.vector.tensor_tensor(
+                out=prod[:].rearrange("p j c -> p (j c)"), in0=h1[:].rearrange("p j c -> p (j c)"), in1=h2_sb, op=MULT
+            )
+            return [(prod[:, jj, :], h3_sb[:, jj, :]) for jj in range(2)]
 
-        def turn_back(a, first, t, u, turned):
-            cols = slice((t - first) * P, (t - first + 1) * P)
+        def turn_back(a, t, u, turned):
+            cols = slice((t % 2) * P, (t % 2 + 1) * P)
             bank = psum.tile([P, BANK], F32, name="by_scalar")
             for jj in range(4):
                 prod, h3_sb = turned[4 * u + jj]
@@ -209,46 +212,53 @@ def tile_list_mycorrhiza_transfer_score_kernel(
         every = slice(0, M)
         halves = [slice(0, M // 2), slice(M // 2, M)]
         w4_raw = [load_raw(w4[a * PASS : (a + 1) * PASS, :]) for a in range(2)]
-        direct_sums(0, direct_products(0))
-        parts = direct_products(1)
-        low = turned_products(0, 2, 0, w1_q0, w3_q0)
+        prods = [direct_product(0, 0), direct_product(0, 1)]
+        direct_sum(0, 0, prods[0])
+        direct_sum(0, 1, prods[1])
+        prods += [direct_product(1, 0), direct_product(1, 1)]
         pick(xa, wa, idx2, 0, 0)
-        direct_sums(1, parts)
-        low += turned_products(0, 2, 1, w1_q0, w3_q0)
+        direct_sum(1, 0, prods[2])
+        direct_sum(1, 1, prods[3])
+
+        unit = turned_products(0, 1, 0)
+        unit += turned_products(0, 1, 1)
         pick(xb, wb, idx3, 0, 0)
-        low += turned_products(0, 2, 2, w1_q0, w3_q0)
-        turn_back(0, 2, 2, 0, low)
-        low += turned_products(0, 2, 3, w1_q0, w3_q0)
-        turn_back(0, 2, 2, 1, low)
-        w1_g1 = round_dealt(w1_raw1)
-        turn_back(0, 2, 3, 0, low)
-        turn_back(0, 2, 3, 1, low)
-        w3_g1 = round_dealt(w3_raw1)
-        pick(xa, wa, idx2, 0, 1)
-        pick(xb, wb, idx3, 0, 1)
-        w1_q1 = quantise("w1_1", w1_g1)
-        pick(xa, wa, idx2, 0, 2)
-        w3_q1 = quantise("w3_1", w3_g1)
-        pick(xb, wb, idx3, 0, 2)
-        high = turned_products(1, 0, 0, w1_q1, w3_q1)
-        pick(xa, wa, idx2, 0, 3)
-        high += turned_products(1, 0, 1, w1_q1, w3_q1)
-        pick(xb, wb, idx3, 0, 3)
-        high += turned_products(1, 0, 2, w1_q1, w3_q1)
-        high += turned_products(1, 0, 3, w1_q1, w3_q1, held("zm", [P, 1, BANK], F32))
-        zm0 = join(MAX, every, "zm")
-        for t in range(2):
-            high += turned_products(1, 0, 4 + t, w1_q1, w3_q1)
-            turn_back(1, 0, t, 0, high)
-        zm0_q = quantise("zm0", zm0)
-        high += turned_products(1, 0, 6, w1_q1, w3_q1)
-        high += turned_products(1, 0, 7, w1_q1, w3_q1, held("zp", [P, 1, BANK], F32))
-        turn_back(1, 0, 0, 1, high)
-        turn_back(1, 0, 1, 1, high)
+        unit += turned_products(0, 1, 2, xb[:, 1, :])
+        unit += turned_products(0, 1, 3, xa[:, 1, :])
+        dealt = [round_dealt(raw, 0) for raw in (w1_raw1, w3_raw1)]
+        w1_q[1, 0] = quantise("w1_10", dealt[0])
         for t in range(2, 4):
             for u in range(2):
-                turn_back(1, 0, t, u, high)
+                turn_back(0, t, u, unit)
+        pick(xa, wa, idx2, 0, 1)
+        w3_q[1, 0] = quantise("w3_10", dealt[1])
+        pick(xb, wb, idx3, 0, 1)
+        pick(xa, wa, idx2, 0, 2)
+        pick(xb, wb, idx3, 0, 2)
+
+        unit = turned_products(1, 0, 0)
+        unit += turned_products(1, 0, 1, xa[:, 3, :])
+        pick(xa, wa, idx2, 0, 3)
+        unit += turned_products(1, 0, 2, xb[:, 3, :])
+        pick(xb, wb, idx3, 0, 3)
+        unit += turned_products(1, 0, 3, held("zm", [P, BANK], F32)[:])
+        dealt = [round_dealt(raw, 1) for raw in (w1_raw1, w3_raw1)]
+        w1_q[1, 1] = quantise("w1_11", dealt[0])
+        w3_q[1, 1] = quantise("w3_11", dealt[1])
+        for t in range(2):
+            for u in range(2):
+                turn_back(1, t, u, unit)
+        zm0 = join(MAX, every, "zm")
+
+        unit = turned_products(1, 1, 0)
+        zm0_q = quantise("zm0", zm0)
+        unit += turned_products(1, 1, 1, held("zp", [P, BANK], F32)[:])
         zp0 = join(MULT, every, "zp")
+        unit += turned_products(1, 1, 2, xb[:, 1, :])
+        unit += turned_products(1, 1, 3, xa[:, 1, :])
+        for t in range(2, 4):
+            for u in range(2):
+                turn_back(1, t, u, unit)
         w4_g = [round_plain(raw) for raw in w4_raw]
 
         y = [[psum.tile([P, M // 2], F32, name=name) for n in range(N // P)] for name in ("by_vector", "by_scalar")]
@@ -273,9 +283,9 @@ def tile_list_mycorrhiza_transfer_score_kernel(
             pick(xb, wb, idx3, 1, t)
         w4_q1 = quantise("w4_1", w4_g[1])
         pick(xa, wa, idx2, 1, PACK - 1)
-        zp0_q = quantise("zp0", zp0)
+        zp0_q = quantise("zp0", zp0, "h1_2")
         pick(xb, wb, idx3, 1, PACK - 1)
-        w4_q0 = quantise("w4_0", w4_g[0])
+        w4_q0 = quantise("w4_0", w4_g[0], "h1_3")
         for u in range(2):
             score_pass(u, *w5_q[0], zp0_q, halves[u], True, False)
         for u in range(2):

from contextlib import ExitStack

import concourse.mybir as mybir
from concourse.masks import make_identity

K, H, N, T, S, M = 512, 1024, 512, 4096, 1024, 512
FLOPS = 2 * K * H * S * 3 + 2 * H * N * M * 2

F32 = mybir.dt.float32
BF16 = mybir.dt.bfloat16
I32 = mybir.dt.int32
U32 = mybir.dt.uint32
U16 = mybir.dt.uint16
U8 = mybir.dt.uint8
E4M3 = mybir.dt.float8_e4m3fn_x4
E2M1 = mybir.dt.float4_e2m1fn_x4
MULT = mybir.AluOpType.mult
ADD = mybir.AluOpType.add
MAX = mybir.AluOpType.max
GELU = mybir.ActivationFunctionType.Gelu_apprx_tanh

P = 128
PACK = 4
PASS = P * PACK
BANK = 512


def tile_list_mycorrhiza_transfer_score_kernel(
    tc, tab_words, tab_scales, offs, w1, w2_words, w2_scales, w3, offs2, offs3, wga, wgb, w4, w5_words, w5_scales, b, out
):
    nc = tc.nc
    with ExitStack() as ctx:
        keep = ctx.enter_context(tc.tile_pool(name="keep", bufs=1))
        ring = ctx.enter_context(tc.tile_pool(name="ring", bufs=2))
        raws = ctx.enter_context(tc.tile_pool(name="raws", bufs=4))
        psum = ctx.enter_context(tc.psum_pool(name="psum", bufs=4))

        def held(name, shape, dtype):
            return keep.tile(shape, dtype, name=name, align_bytes=64)

        def load_scale_rows(queue, plane, rows):
            for q in range(4):
                queue.dma_start(out=plane[32 * q : 32 * q + 4], in_=rows[4 * q : 4 * q + 4])

        def load_raw(rows):
            raw = raws.tile([P, PACK, BANK], F32, name="raw")
            nc.sync.dma_start(out=raw[:], in_=rows.rearrange("(p j) c -> p j c", j=PACK))
            return raw

        def round_plain(raw):
            grouped = ring.tile([P, BANK, PACK], BF16, name="grouped", align_bytes=64)
            nc.scalar.copy(
                out=grouped[:].rearrange("p (c i) j -> p c j i", i=4),
                in_=raw[:].rearrange("p j (c i) -> p c j i", i=4),
            )
            return grouped

        def round_dealt(raw, pair):
            grouped = ring.tile([P, 2 * P, PACK], BF16, name="dealt", bufs=4, align_bytes=64)
            nc.scalar.copy(
                out=grouped[:].rearrange("p (t m) j -> p m j t", t=2),
                in_=raw[:].rearrange("p j (m t) -> p m j t", t=PACK)[:, :, :, 2 * pair : 2 * pair + 2],
            )
            return grouped

        def quantise(name, grouped, codes_name=None):
            width = grouped.shape[1]
            codes = held(codes_name or name + "_codes", [P, width], U32)
            scales = held(name + "_scales", [P, width], U8)
            nc.vector.quantize_mx(
                out=codes[:].bitcast(E4M3), scales=scales[:], in_=grouped[:].rearrange("p c j -> p (c j)")
            )
            return codes, scales

        idx = held("idx", [P, S // 16], U16)
        idx2 = held("idx2", [P, M // 16], U16)
        idx3 = held("idx3", [P, M // 16], U16)
        tab_w = held("tab_w", [P, T], I32)
        tab_s = held("tab_s", [P, T // 4], I32)
        w2_w = held("w2_w", [P, 2 * H // 4], I32)
        w2_s = held("w2_s", [P, H // 4], I32)
        w5_w = held("w5_w", [P, 2, N], I32)
        w5_s = held("w5_s", [P, 2, N // 4], I32)
        wa = held("wa", [P, M], F32)
        wb = held("wb", [P, M], F32)
        bias = held("bias", [P, N // P], F32)
        ident = held("ident", [P, P], F32)

        nc.vector.memset(tab_s[:], 0)
        nc.gpsimd.memset(w2_s[:], 0)
        nc.gpsimd.memset(w5_s[:], 0)
        make_identity(nc, ident[:])
        w1_raw0 = load_raw(w1[:, 0:BANK])
        load_scale_rows(nc.sync, tab_s, tab_scales[0].bitcast(I32))
        nc.sync.dma_start(out=idx[:], in_=offs)
        w3_raw0 = load_raw(w3[:, 0:BANK])
        nc.sync.dma_start(out=w2_w[:], in_=w2_words[0].bitcast(I32))
        load_scale_rows(nc.sync, w2_s, w2_scales[0].bitcast(I32))
        nc.sync.dma_start(out=tab_w[:], in_=tab_words[0].rearrange("p t i -> p (t i)").bitcast(I32))
        nc.sync.dma_start(out=idx2[:], in_=offs2)
        nc.sync.dma_start(out=idx3[:], in_=offs3)
        nc.sync.dma_start(out=wa[:], in_=wga)
        nc.sync.dma_start(out=wb[:], in_=wgb)
        w1_raw1 = load_raw(w1[:, BANK:H])
        w3_raw1 = load_raw(w3[:, BANK:H])
        nc.sync.dma_start(
            out=w5_w[:], in_=w5_words.rearrange("a p c i -> a p (c i)").bitcast(I32).rearrange("a p c -> p a c")
        )
        load_scale_rows(nc.sync, w5_s, w5_scales.bitcast(I32).rearrange("a q c -> q a c"))
        with nc.allow_non_contiguous_dma(reason="one bias value a partition"):
            nc.sync.dma_start(out=bias[:], in_=b.rearrange("(c p) -> p c", p=P))

        v_s = held("v_s", [P, S], U8)
        nc.vector.tensor_copy(out=v_s[:], in_=tab_s[:].bitcast(U8).indirect(idx[:]))

        w2_dealt_w = held("w2_dealt_w", [P, 2, BANK], U16)
        w2_dealt_s = held("w2_dealt_s", [P, 2, BANK], U8)
        nc.vector.tensor_copy(
            out=w2_dealt_w[:].rearrange("p a (t m) -> p a t m", t=PACK),
            in_=w2_w[:].bitcast(U16).rearrange("p (a m t) -> p a t m", a=2, t=PACK),
        )
        nc.vector.tensor_copy(
            out=w2_dealt_s[:].rearrange("p a (t m) -> p a t m", t=PACK),
            in_=w2_s[:].bitcast(U8).rearrange("p (a m t) -> p a t m", a=2, t=PACK),
        )
        w1_q = {(0, pair): quantise("w1_0%d" % pair, round_dealt(w1_raw0, pair)) for pair in range(2)}
        w3_q = {(0, pair): quantise("w3_0%d" % pair, round_dealt(w3_raw0, pair)) for pair in range(2)}

        v_w = [held("v_w%d" % u, [P, BANK], U32) for u in range(2)]
        for u in range(2):
            nc.vector.tensor_copy(out=v_w[u][:], in_=tab_w[:].bitcast(U32).indirect(idx[:, 32 * u : 32 * u + 32]))

        h = [[held("h%d_%d" % (a, t), [P, S], F32) for t in range(PACK)] for a in range(2)]
        xa = held("xa", [P, PACK, M], F32)
        xb = held("xb", [P, PACK, M], F32)

        def moving_table(u):
            return dict(rhs=v_w[u][:].bitcast(E4M3), rhs_scale=v_s[:, u * BANK : (u + 1) * BANK], start=True, stop=True)

        def direct_product(t, u):
            cols = slice(t * P, (t + 1) * P)
            h2 = psum.tile([P, BANK], F32, name="by_scalar")
            nc.tensor.matmul_mx(
                out=h2[:], lhsT=w2_dealt_w[:, 0, cols].bitcast(E2M1), lhsT_scale=w2_dealt_s[:, 0, cols], **moving_table(u)
            )
            h1 = psum.tile([P, BANK], F32, name="by_vector")
            codes, scales = w1_q[0, 0]
            nc.tensor.matmul_mx(out=h1[:], lhsT=codes[:, cols].bitcast(E4M3), lhsT_scale=scales[:, cols], **moving_table(u))
            h2_sb = ring.tile([P, BANK], F32, name="h2_sb", bufs=4)
            nc.scalar.copy(out=h2_sb[:], in_=h2[:])
            prod = ring.tile([P, BANK], F32, name="prod", bufs=4)
            nc.vector.tensor_tensor(out=prod[:], in0=h1[:], in1=h2_sb[:], op=MULT)
            return prod

        def direct_sum(t, u, prod):
            cols = slice(t * P, (t + 1) * P)
            h3 = psum.tile([P, BANK], F32, name="by_vector")
            codes, scales = w3_q[0, 0]
            nc.tensor.matmul_mx(out=h3[:], lhsT=codes[:, cols].bitcast(E4M3), lhsT_scale=scales[:, cols], **moving_table(u))
            nc.vector.tensor_tensor(out=h[0][t][:, u * BANK : (u + 1) * BANK], in0=h3[:], in1=prod[:], op=ADD)

        def pick(x, weight, lists, a, t):
            nc.vector.tensor_tensor(out=x[:, t, :], in0=h[a][t][:].indirect(lists[:]), in1=weight[:], op=MULT)

        def turned_products(a, pair, r, h2_sb=None):
            cols = slice(pair * 2 * P, (pair + 1) * 2 * P)
            h2 = psum.tile([P, 2, 2 * P], F32, name="by_scalar")
            h1 = psum.tile([P, 2, 2 * P], F32, name="by_vector")
            h3 = psum.tile([P, 2, 2 * P], F32, name="by_scalar")
            for bank, codes, scales in (
                (h2, w2_dealt_w[:, a, cols].bitcast(E2M1), w2_dealt_s[:, a, cols]),
                (h1, w1_q[a, pair][0][:].bitcast(E4M3), w1_q[a, pair][1][:]),
                (h3, w3_q[a, pair][0][:].bitcast(E4M3), w3_q[a, pair][1][:]),
            ):
                for jj in range(2):
                    j = 2 * r + jj
                    nc.tensor.matmul_mx(
                        out=bank[:, jj, :], lhsT=v_w[j // 4][:, (j % 4) * P : (j % 4 + 1) * P].bitcast(E4M3),
                        lhsT_scale=v_s[:, j * P : (j + 1) * P], rhs=codes, rhs_scale=scales, start=True, stop=True,
                    )
            if h2_sb is None:
                h2_sb = ring.tile([P, BANK], F32, name="h2_sb", bufs=4)[:]
            nc.scalar.copy(out=h2_sb, in_=h2[:].rearrange("p j c -> p (j c)"))
            h3_sb = keep.tile([P, 2, 2 * P], F32, name="h3_turned", bufs=8)
            nc.scalar.copy(out=h3_sb[:], in_=h3[:])
            prod = keep.tile([P, 2, 2 * P], F32, name="prod_turned", bufs=8)
            nc.vector.tensor_tensor(
                out=prod[:].rearrange("p j c -> p (j c)"), in0=h1[:].rearrange("p j c -> p (j c)"), in1=h2_sb, op=MULT
            )
            return [(prod[:, jj, :], h3_sb[:, jj, :]) for jj in range(2)]

        def turn_back(a, t, u, turned):
            cols = slice((t % 2) * P, (t % 2 + 1) * P)
            bank = psum.tile([P, BANK], F32, name="by_scalar")
            for jj in range(4):
                prod, h3_sb = turned[4 * u + jj]
                dst = bank[:, jj * P : (jj + 1) * P]
                nc.tensor.matmul(out=dst, lhsT=h3_sb[:, cols], rhs=ident[:], is_transpose=True, start=True, stop=False)
                nc.tensor.matmul(out=dst, lhsT=prod[:, cols], rhs=ident[:], is_transpose=True, start=False, stop=True)
            nc.scalar.copy(out=h[a][t][:, u * BANK : (u + 1) * BANK], in_=bank[:])

        def join(op, cols, name):
            z = held(name, [P, cols.stop - cols.start, PACK], BF16)
            nc.vector.tensor_tensor(
                out=z[:].rearrange("p (c i) t -> p c t i", i=4),
                in0=xa[:, :, cols].rearrange("p t (c i) -> p c t i", i=4),
                in1=xb[:, :, cols].rearrange("p t (c i) -> p c t i", i=4),
                op=op,
            )
            return z

        every = slice(0, M)
        halves = [slice(0, M // 2), slice(M // 2, M)]
        w4_raw = [load_raw(w4[a * PASS : (a + 1) * PASS, :]) for a in range(2)]
        prods = [direct_product(0, 0), direct_product(0, 1)]
        direct_sum(0, 0, prods[0])
        direct_sum(0, 1, prods[1])
        prods += [direct_product(1, 0), direct_product(1, 1)]
        pick(xa, wa, idx2, 0, 0)
        direct_sum(1, 0, prods[2])
        direct_sum(1, 1, prods[3])

        unit = turned_products(0, 1, 0)
        unit += turned_products(0, 1, 1)
        pick(xb, wb, idx3, 0, 0)
        unit += turned_products(0, 1, 2, xb[:, 1, :])
        unit += turned_products(0, 1, 3, xa[:, 1, :])
        dealt = [round_dealt(raw, 0) for raw in (w1_raw1, w3_raw1)]
        w1_q[1, 0] = quantise("w1_10", dealt[0])
        for t in range(2, 4):
            for u in range(2):
                turn_back(0, t, u, unit)
        pick(xa, wa, idx2, 0, 1)
        w3_q[1, 0] = quantise("w3_10", dealt[1])
        pick(xb, wb, idx3, 0, 1)
        pick(xa, wa, idx2, 0, 2)
        pick(xb, wb, idx3, 0, 2)

        unit = turned_products(1, 0, 0)
        unit += turned_products(1, 0, 1, xa[:, 3, :])
        pick(xa, wa, idx2, 0, 3)
        unit += turned_products(1, 0, 2, xb[:, 3, :])
        pick(xb, wb, idx3, 0, 3)
        unit += turned_products(1, 0, 3, held("zm", [P, BANK], F32)[:])
        dealt = [round_dealt(raw, 1) for raw in (w1_raw1, w3_raw1)]
        w1_q[1, 1] = quantise("w1_11", dealt[0])
        w3_q[1, 1] = quantise("w3_11", dealt[1])
        for t in range(2):
            for u in range(2):
                turn_back(1, t, u, unit)
        zm0 = join(MAX, every, "zm")

        unit = turned_products(1, 1, 0)
        zm0_q = quantise("zm0", zm0)
        unit += turned_products(1, 1, 1, held("zp", [P, BANK], F32)[:])
        zp0 = join(MULT, every, "zp")
        unit += turned_products(1, 1, 2, xb[:, 1, :])
        unit += turned_products(1, 1, 3, xa[:, 1, :])
        for t in range(2, 4):
            for u in range(2):
                turn_back(1, t, u, unit)
        w4_g = [round_plain(raw) for raw in w4_raw]

        y = [[psum.tile([P, M // 2], F32, name=name) for n in range(N // P)] for name in ("by_vector", "by_scalar")]

        def score_pass(u, w_codes, w_scales, z_q, z_cols, start, stop):
            for n in range(N // P):
                cols = slice(n * P, (n + 1) * P)
                nc.tensor.matmul_mx(
                    out=y[u][n][:], lhsT=w_codes[:, cols].bitcast(E4M3), lhsT_scale=w_scales[:, cols],
                    rhs=z_q[0][:, z_cols].bitcast(E4M3), rhs_scale=z_q[1][:, z_cols], start=start, stop=stop,
                )

        def finish(u):
            for n in range(N // P):
                res = raws.tile([P, M // 2], F32, name="res", bufs=8)
                nc.scalar.activation(out=res[:], in_=y[u][n][:], func=GELU, bias=bias[:, n : n + 1])
                nc.sync.dma_start(out=out[n * P : (n + 1) * P, halves[u]], in_=res[:])

        w5_q = [(w5_w[:, a, :], w5_s[:, a, :].bitcast(U8)) for a in range(2)]
        for t in range(PACK - 1):
            pick(xa, wa, idx2, 1, t)
            pick(xb, wb, idx3, 1, t)
        w4_q1 = quantise("w4_1", w4_g[1])
        pick(xa, wa, idx2, 1, PACK - 1)
        zp0_q = quantise("zp0", zp0, "h1_2")
        pick(xb, wb, idx3, 1, PACK - 1)
        w4_q0 = quantise("w4_0", w4_g[0], "h1_3")
        for u in range(2):
            score_pass(u, *w5_q[0], zp0_q, halves[u], True, False)
        for u in range(2):
            score_pass(u, *w4_q0, zm0_q, halves[u], False, False)
        zm1 = join(MAX, every, "zm")
        zp1 = join(MULT, halves[0], "zp")
        zm1_q = quantise("zm1", zm1)
        zp1_q = quantise("zp1a", zp1)
        score_pass(0, *w4_q1, zm1_q, halves[0], False, False)
        score_pass(0, *w5_q[1], zp1_q, halves[0], False, True)
        finish(0)
        score_pass(1, *w4_q1, zm1_q, halves[1], False, False)
        zp1_q = quantise("zp1b", join(MULT, halves[1], "zp_last"))
        score_pass(1, *w5_q[1], zp1_q, halves[0], False, True)
        finish(1)
